import numpy as np, ml_dtypes
CORES = [2,6,10,14,18,22,26,30]
N = 8
BF = ml_dtypes.bfloat16
def gentries(a):
    return np.ascontiguousarray(a.reshape(8, 16, -1).transpose(0, 2, 1)).reshape(8, -1)
def gtable(e):
    e = np.asarray(e); return np.ascontiguousarray(e.reshape(8, -1, 16).transpose(0, 2, 1)).reshape(128, -1).astype(np.int32)
W, P, S, V, Q, F = 4096, 512, 8, 5, 8, 4096
def parts(rng):
    return (rng.integers(0, 256, (N, 8, 16, W)), rng.integers(0, W, (N, 8, P, S)), rng.integers(0, W, (N, 8, P, S)), rng.integers(0, S + 1, (N, 8, P)),
            rng.integers(0, S + 1, (N, 8, P)), rng.integers(600, 1201, (N, 8, P)), rng.integers(0, 16, (N, 8, 16)))
def first(h, m):
    return np.where(m > 0, h[..., 0], (37 * np.arange(P)) & (F - 1))
def pack(x, h, t, m, n, th, w):
    return {"x0": np.ascontiguousarray(x.reshape(N, 128, W)).astype(np.float32).astype(BF), "hands": np.stack([gtable(a.reshape(8, -1)) for a in h]), "trains": np.stack([gtable(a.reshape(8, -1)) for a in t]),
            "mh": m.astype(np.int32), "nt": n.astype(np.int32), "th": th.astype(np.int32), "wt": np.ascontiguousarray(w.reshape(N, 128, 1)).astype(np.int32)}
def setup_inputs(rng):
    return pack(*parts(rng))
def setup_inputs_spread(rng):
    x, h, t, m, n, th, w = parts(rng)
    x = np.minimum((np.exp2(8 * rng.random((N, 8, 1, W))) * rng.random((N, 8, 16, W))).astype(np.int64), 255)
    h = np.minimum((W * rng.random(h.shape) ** 3).astype(np.int64), W - 1); t = W - 1 - np.minimum((W * rng.random(t.shape) ** 2).astype(np.int64), W - 1)
    m = np.minimum(((S + 1) * rng.random(m.shape) ** 2).astype(np.int64), S); n = S - np.minimum(((S + 1) * rng.random(n.shape) ** 2).astype(np.int64), S)
    th = np.minimum(np.exp2(12 * rng.random(th.shape)).astype(np.int64) - 1, 4080)
    return pack(x, h, t, m, n, th, w)
def setup_inputs_ends(rng):
    x, h, t, m, n, th, w = parts(rng); e = W - 1; q = N - 1
    x = 255 * rng.integers(0, 2, (N, 8, 16, W)); x = np.where(rng.random((N, 8, 1, W)) < 0.25, x[:, :, :1, :], x)
    for g, b in enumerate((0, 1, 2, 1, 0, 2, 1, 0)):
        if b < 2: x[:, g, :, 0] = 255 * b
    x[:, :, :, e] = 255 - x[:, :, :, 0]
    h = np.where(rng.random(h.shape) < 0.8, e * rng.integers(0, 2, h.shape), h); t = np.where(rng.random(t.shape) < 0.8, e * rng.integers(0, 2, t.shape), t)
    m = np.where(rng.random(m.shape) < 0.85, S * rng.integers(0, 2, m.shape), m); n = np.where(rng.random(n.shape) < 0.85, S * rng.integers(0, 2, n.shape), n)
    th = np.where(rng.random(th.shape) < 0.8, 4080 * rng.integers(0, 2, th.shape), np.maximum(255 * rng.integers(0, 17, th.shape) - rng.integers(0, 2, th.shape), 0))
    w = 15 * rng.integers(0, 2, w.shape); w[:, 0] = 15; w[:, 7] = 15; w[:, 3] = 0
    a = rng.integers(0, 2, (8, P - 8))
    h[q, :, 8:, 0] = e * a; t[q, :, 8:, 0] = e * a; t[q, :, 8:, 1:] = (e * (1 - a))[:, :, None]
    m[q, :, 8:] = S; n[q, :, 8:] = S; th[q, :, 8:] = 0
    th[q, :, 2] = 4080; n[q, :, 2] = S; m[q, :, 3] = 0; n[q, :, 3] = 0
    h[q, 7, P - 1, 0] = e; n[q, 7, P - 1] = 0
    h[q, 7, 1, 0] = e; t[q, 7, 1] = 0; m[q, 7, 1] = S; n[q, 7, 1] = S; th[q, 7, 1] = 0
    return pack(x, h, t, m, n, th, w)
def setup_inputs_corners(rng):
    x, h, t, m, n, th, w = parts(rng)
    kd = rng.integers(0, 10, (N, 8, P)); kd[:, :, :10] = np.arange(10); kd[:, :, P - 10:] = np.arange(10)
    kd[0] = rng.choice(np.array([1, 4, 6]), (8, P)); kd[1] = rng.choice(np.array([0, 2, 3]), (8, P))
    kd[0, 2, 5] = 5; kd[0, 7, P - 1] = 0
    m = np.array([0, 0, S, S, 1, 1, S, 2, S - 1, 3])[kd]; n = np.array([0, S, 0, S, S, S - 1, S, S, S, 1])[kd]
    c = np.where(m > 0, h[..., 0], (37 * np.arange(P)) & (F - 1))
    t = (c[..., None] + rng.integers(1, W, t.shape)) % W; s = np.arange(S); k = kd[..., None]
    own = (((k == 1) | (k == 4) | (k == 5) | (k == 6)) & (s == 0)) | ((k == 7) & (s == S - 1)) | ((k == 8) & ((s == 3) | (s == 5))) | (k == 9)
    t = np.where(own, c[..., None], t)
    th = np.where((kd == 0) | (kd == 2), rng.choice(np.array([0, 1, 4079, 4080]), th.shape), 0)
    w[:, 1] = 0; w[:, 3] = 15; w[:, 5] = 0; w[:, 5, 15] = 1; w[:, 6] = 0; w[:, 6, 0] = 15
    return pack(x, h, t, m, n, th, w)
def setup_inputs_ties(rng):
    x, h, t, m, n, th, w = parts(rng)
    x = 4 * rng.integers(0, 64, (N, 8, 1, W)) + np.zeros((1, 1, 16, 1), np.int64)
    x[:, ::2] = x[:, ::2] + rng.integers(0, 2, (N, 4, 16, W)) * (rng.random((N, 4, 1, W)) < 0.25)
    th = np.maximum(64 * rng.integers(0, 12, th.shape) + rng.integers(-1, 2, th.shape), 0)
    t[:, 1::2] = np.where(rng.random((N, 4, P, S)) < 0.15, h[:, 1::2, :, :1], t[:, 1::2])
    t[:, 2] = rng.choice(np.array([0, 1, W - 2, W - 1]), (N, P, S)); h[:, 4] = rng.choice(np.array([0, 7, W - 1]), (N, P, S)); t[:, 6] = t[:, 6, :, :1]
    a = np.maximum(n[1], 1).reshape(-1); a[rng.permutation(8 * P)[:256]] = 0; n[1] = a.reshape(8, P)
    t[1] = np.where(np.arange(S) == n[1][..., None] - 1, first(h[1], m[1])[..., None], t[1])
    return pack(x, h, t, m, n, th, w)
def setup_inputs_counts(rng):
    x, h, t, m, n, th, w = parts(rng); b = N - 1; D = min(N - 3, V - 2, 3); p = b - D; s = np.arange(S)
    x[:2, 7] = np.where(np.arange(W) % 2 == 0, rng.integers(250, 256, (2, 16, W)), rng.integers(0, 10, (2, 16, W))); w[0, 7] = 15
    m[0, 1] = 0; n[0] = S
    m[1, 2] = 0; n[1] = np.maximum(n[1], 1); n[1, 2] = 0; n[1, 3, rng.permutation(P)[:99]] = 0
    c = first(h, m)
    t[:2] = (c[:2, ..., None] + 1 + 2 * rng.integers(0, W // 2, (2, 8, P, S))) % W
    t[0, ..., 0] = c[0]
    t[1, :7] = np.where(s == n[1, :7, :, None] - 1, c[1, :7, :, None], t[1, :7])
    XT = np.take_along_axis(x[:2], t[:2].reshape(2, 8, 1, P * S), 3).reshape(2, 8, 16, P, S); XC = np.take_along_axis(x[:2], c[:2, :, None, :], 3)
    d = np.add.reduce(np.abs(XT - XC[..., None]), axis=2)
    th[0] = np.maximum(np.min(d[0, ..., 1:], axis=-1) - 1, 0)
    th[1, 7] = np.take_along_axis(d[1, 7], n[1, 7][:, None] - 1, 1)[:, 0]
    th[p:] = 0; n[p:] = np.maximum(n[p:], 1); n[p] = S - D
    t[p:] = 8 * rng.integers(0, W // 8, (N - p, 8, P, S)); t[p, ..., 1:] = (t[p, ..., :1] + 8 * rng.integers(1, W // 8, (8, P, S - 1))) % W
    t[p:, :, P - 2:] = t[p:, :, P - 2:] + 4
    for u in range(D):
        h[p + u] = 8 * rng.integers(0, W // 8, (8, P, S)) + 1 + u; m[p + u] = rng.integers(D, S + 1, (8, P))
    h[b] = 8 * rng.integers(0, W // 8, (8, P, S)) + 7; h[b, ..., D] = np.roll(t[p, ..., 0], D, axis=0)
    m[b] = rng.integers(D + 1, S + 1, (8, P)); m[b, :, P - 2:] = 0
    return pack(x, h, t, m, n, th, w)
def check_inputs(d):
    bad = []
    for k, lo, hi in (("x0", 0, 255), ("hands", 0, W - 1), ("trains", 0, W - 1), ("mh", 0, S), ("nt", 0, S), ("th", 0, 4080), ("wt", 0, 15)):
        v = np.asarray(d[k]).astype(np.float64)
        if not (np.min(v) >= lo and np.max(v) <= hi): bad.append("range of " + k)
        elif np.any(v != np.rint(v)): bad.append("whole numbers of " + k)
    return bad
def reference(x0, hands, trains, mh, nt, th, wt):
    X = x0.astype(np.float32).astype(np.int32).reshape(N, 8, 16, W); s = np.arange(S); i = np.arange(P)
    H = np.stack([gentries(a) for a in hands]).astype(np.int64).reshape(N, 8, P, S); T = np.stack([gentries(a) for a in trains]).astype(np.int64).reshape(N, 8, P, S)
    m = mh.astype(np.int64); n = nt.astype(np.int64); lim = th.astype(np.int64); wv = wt.astype(np.int64).reshape(N, 8, 16, 1)
    H = np.where(s < m[..., None], H, 0); T = np.where(s < n[..., None], T, 0)
    A = np.zeros(N, np.int64); zero = np.zeros((N, 8, P, 1), np.int64)
    for t in range(V):
        if t > 0:
            j = 1 + t // N - (t - 1) // N
            T = np.roll(T, (1, j), axis=(0, 1)); n = np.roll(n, (1, j), axis=(0, 1))
        A3 = A[:, None, None]
        c = np.where(m > 0, H[..., 0], (37 * i + 613 * t + A3) & (F - 1))
        H = np.concatenate([H[..., 1:], zero], axis=-1); m = np.maximum(m - 1, 0)
        XT = np.take_along_axis(X, T.reshape(N, 8, 1, P * S), 3).reshape(N, 8, 16, P, S); XC = np.take_along_axis(X, c[:, :, None, :], 3)
        dist = np.add.reduce(np.abs(XT - XC[..., None]), axis=2)
        ok = (dist <= (lim + (A3 & 255))[..., None]) & (s < n[..., None])
        k = np.max(np.where(ok, s, -1), axis=-1); hit = k >= 0; got = np.where(hit, n - k, 0)
        XS = np.take_along_axis(XT, np.maximum(k, 0)[:, :, None, :, None], 4)[..., 0]
        y = np.where(hit[:, :, None, :], (XC + XS) >> 1, np.where((n == 0)[:, :, None, :], XC, np.abs(XC - XS)))
        z = np.add.reduce(wv * y, axis=2) & (Q - 1)
        np.put_along_axis(X, (Q * i + z)[:, :, None, :], y, 3)
        h1 = hit[..., None]; m1 = m[..., None]; c1 = c[..., None]; n1 = n[..., None]
        back = np.take_along_axis(T, np.clip(m1 + n1 - s, 0, S - 1), 3)
        H = np.where(h1 & (s == m1), c1, np.where(h1 & (s > m1) & (s <= m1 + got[..., None]), back, H))
        m = np.where(hit, np.minimum(m + 1 + got, S), m)
        grown = np.where(n1 == S, np.concatenate([T[..., 1:], zero], axis=-1), T)
        grown = np.where(s == np.minimum(n1, S - 1), c1, grown)
        T = np.where(h1, np.where(s < k[..., None], T, 0), grown); n = np.where(hit, k, np.minimum(n + 1, S))
        A = np.sum(got, axis=(1, 2))
    return {"yx": X.reshape(N, 128, W).astype(np.float32).astype(BF), "yh": np.stack([gtable(a.reshape(8, -1)) for a in H]).astype(np.float32), "yt": np.stack([gtable(a.reshape(8, -1)) for a in T]).astype(np.float32),
            "ym": m.astype(np.float32), "yn": n.astype(np.float32)}

from concourse.mybir import AluOpType, AxisListType, ActivationFunctionType

V = 5
WX = 4096
ZEROC, BIGC = 4096, 4097
GB = 4112
WW = GB + 512
NL = 288
VS = [0, 1, 2]

SCRATCH = {
    "DMm": ("dram", [8, 1024], "int32"), "DMn": ("dram", [8, 1024], "int32"), "DMh": ("dram", [8, 1024], "int32"),
    "DYm": ("dram", [8, 1024], "float32"), "DYn": ("dram", [8, 1024], "float32"),
}


def _declare(dtype, cols, names):
    for nm in names.split():
        SCRATCH[nm] = ("sbuf", [128, cols], dtype)


_declare("bfloat16", WW, "XW")
_declare("bfloat16", 4096, "XT DA")
_declare("bfloat16", 2048, "LL")
_declare("float16", 2048, "LW")
_declare("bfloat16", 512, "XC Y")
_declare("float32", 512, "XCM")
_declare("float16", 512, "VV")
_declare("bfloat16", 256, "ONE2 NSC RR0 RR1 RR2 RR3 RRC")
_declare("bfloat16", 128, "ONES BGA BGB IDN NID SEL0 SEL1 Q1 Q2 Q3 QT1 QT2 QN2 QT3")
_declare("float32", 416, "H")
_declare("float32", NL, "TF")
_declare("float32", 256, "TS DSH TN KEY HD X1 B1 BA BB SC7 KC CUT OH OT OG")
_declare("bfloat16", 256, "CNB")
_declare("bfloat16", 128, "ID2")
_declare("bfloat16", 64, "THH THL")
_declare("float32", 1, "SCA NSCA P5 S5")
_declare("int32", 1, "P5I S5I")
_declare("int32", 256, "HI TI")
_declare("int32", 192, "M2")
_declare("float32", 192, "OKW")
_declare("float32", 96, "ME MO MNT")
_declare("int32", 96, "FB")
_declare("float32", 64, "OKK MX YMB YNB")
_declare("bfloat16", 64, "MNB")
_declare("float32", 32, "A2")
ALIAS = {}
for _buf, _dt, _names in (("SMALLF", "float32", "IF I8 C37 GK MP DF CF M V0 HIT G1 N1 N9 NN NF MA MB ZF"),
                          ("SMALLI", "int32", "CDI CD FI KI KS K1 ZI ZJ")):
    for _k, _nm in enumerate(_names.split()):
        ALIAS[_nm] = (_buf, 32 * _k)
    _declare(_dt, 32 * len(_names.split()), _buf)
_declare("uint16", 32, "CU SU ZU")
_declare("bfloat16", 32, "GOT")
_declare("float32", 1, "WF UF BF NBF LF IB AC A255")
_declare("int32", 1, "WI PI UI BI LI AI AJ")
for _t in range(V):
    _declare("uint16", NL, "TL%d TO%d" % (_t, _t))
for _b in range(8):
    SCRATCH["ps%d" % _b] = ("psum", [128, 512], "float32")
GROUPS = ["lx", "lm1", "lm2", "lh", "lt", "lw", "ox", "oh", "ot", "om1", "om2"]
SEMAPHORES = ["e_v", "e_s", "e_t", "e_g"] + GROUPS + ["rx%d" % t for t in range(1, V)] + ["tx%d" % t for t in range(1, V)]

ADD, SUB, MUL, MAX, MIN = AluOpType.add, AluOpType.subtract, AluOpType.mult, AluOpType.max, AluOpType.min
GEQ, GT, LE, LT, EQ, NE = AluOpType.is_ge, AluOpType.is_gt, AluOpType.is_le, AluOpType.is_lt, AluOpType.is_equal, AluOpType.not_equal
AND, SHR = AluOpType.bitwise_and, AluOpType.logical_shift_right
AF = ActivationFunctionType


def rank_program(g, core, T, topo):
    rank = T.rank_of(core)
    if rank is None:
        return
    n_ranks = len(T.cores)
    queues = {"v": g.vector, "s": g.scalar, "t": g.tensor, "g": g, "y": g.sync}

    ops = []

    def rec(q, fn, reads, writes, group=None, inc=16):
        ops.append({"q": q, "fn": fn, "r": [x for x in reads if x is not None], "w": writes, "grp": group, "inc": inc})

    def ap(r):
        return T[r[0]][:, r[1]:r[2]] if r[3] == 1 else T[r[0]][:, r[1]:r[2]:r[3]]

    def R(name, lo=0, hi=None, st=1):
        if name in ALIAS:
            return (ALIAS[name][0], ALIAS[name][1], ALIAS[name][1] + 32, 1)
        return (name, lo, SCRATCH[name][1][1] if hi is None else hi, st)

    def S(name, s):
        return R(name, 32 * s, 32 * s + 32)

    def val(x):
        return ap(x) if isinstance(x, tuple) else x

    def reg(x):
        return x if isinstance(x, tuple) else None

    def ts(out, in0, s1, op0, s2=None, op1=None):
        if op1 is None:
            rec("v", lambda: g.vector.tensor_scalar(ap(out), ap(in0), val(s1), None, op0), [in0, reg(s1)], [out])
        else:
            rec("v", lambda: g.vector.tensor_scalar(ap(out), ap(in0), val(s1), val(s2), op0, op1), [in0, reg(s1), reg(s2)], [out])

    def tt(out, a, b, op):
        rec("v", lambda: g.vector.tensor_tensor(ap(out), ap(a), ap(b), op), [a, b], [out])

    def cp(out, a):
        rec("v", lambda: g.vector.tensor_copy(ap(out), ap(a)), [a], [out])

    def fill(out, c):
        rec("v", lambda: g.vector.memset(ap(out), c), [], [out])

    def act(out, in_, func, **kw):
        rec("s", lambda: g.scalar.activation(ap(out), ap(in_), func, **{k: val(kw[k]) for k in kw}), [in_] + [reg(kw[k]) for k in kw], [out])

    def mms(calls):
        def fn():
            last = None
            for k, (o, a, b) in enumerate(calls):
                last = g.tensor.matmul(ap(o), ap(a), ap(b), k == 0, k == len(calls) - 1)
            return last
        rec("t", fn, [c[1] for c in calls] + [c[2] for c in calls], [calls[0][0]])

    def dma(q, group, out, in_, reads, writes):
        rec(q, lambda: queues[q].dma_start(out, in_), reads, writes, group)

    sh = rank % 8
    pieces = [(0, sh, 8 - sh)] + ([(8 - sh, 0, sh)] if sh else [])

    for f, gg, k in pieces:
        for src, nm in ((T.mh, "DMm"), (T.nt, "DMn"), (T.th, "DMh")):
            for b in range(2):
                dma("y", "lm1", T[nm][f:f + k, 512 * b:512 * b + 512], src[gg:gg + k, :], [], [R(nm)])
        dma("s", "lw", T.WI[16 * f:16 * (f + k), :], T.wt[16 * gg:16 * (gg + k), :], [], [R("WI")])
    for s in range(8):
        for f, gg, k in pieces:
            dma("s", "lh", T.HI[16 * f:16 * (f + k), 32 * (7 - s):32 * (8 - s)], T.hands[16 * gg + s:16 * (gg + k):8, :], [], [S("HI", 7 - s)])
            dma("y", "lt", T.TI[16 * f:16 * (f + k), 32 * s:32 * s + 32], T.trains[16 * gg + s:16 * (gg + k):8, :], [], [S("TI", s)])
    for k, nm in enumerate(("DMm", "DMn", "DMh")):
        dma("y", "lm2", T.M2[:, 64 * k:64 * k + 64], T[nm][:, :], [R(nm)], [R("M2", 64 * k, 64 * k + 64)])
    for f, gg, k in pieces:
        dma("y", "lx", T.XW[16 * f:16 * (f + k), 0:WX], T.x0[16 * gg:16 * (gg + k), :], [], [R("XW", 0, WX)])

    fill(R("ONES"), 1.0)
    fill(R("ONE2"), 1.0)
    rec("g", lambda: g.iota(T.PI[:, :], [[0, 1]], 0, 1), [], [R("PI")])
    rec("g", lambda: g.iota(T.A2[:, :], [[2, 32]], 0, 0, allow_small_or_imprecise_dtypes=True), [], [R("A2")])
    rec("g", lambda: g.affine_select(T.BGA[:, :], T.ONES[:, :], [[-16, 8], [0, 16]], GEQ, 0.0, 0, 1), [R("ONES")], [R("BGA")])
    rec("g", lambda: g.affine_select(T.BGB[:, :], T.BGA[:, :], [[16, 8], [0, 16]], GEQ, 0.0, 15, -1), [R("BGA")], [R("BGB")])
    rec("g", lambda: g.affine_select(T.IDN[:, :], T.ONES[:, :], [[-1, 128]], EQ, 0.0, 0, 1), [R("ONES")], [R("IDN")])
    for q in range(4):
        rec("g", lambda q=q: g.affine_select(T["RR%d" % q][:, :], T.ONE2[:, :], [[0, 8], [-1, 32]], EQ, 0.0, -32 * q, 1), [R("ONE2")], [R("RR%d" % q)])
    rec("g", lambda: g.iota(T.NSC[:, :], [[-1, 8], [0, 32]], 0, 0, allow_small_or_imprecise_dtypes=True), [], [R("NSC")])
    rec("g", lambda: g.iota(T.SC7[:, :], [[-1, 8], [0, 32]], 7, 0, allow_small_or_imprecise_dtypes=True), [], [R("SC7")])
    rec("g", lambda: g.iota(T.KC[:, :], [[8192, 8], [0, 32]], 8192, 0, allow_small_or_imprecise_dtypes=True), [], [R("KC")])
    fill(R("LL"), 0.0)
    fill(R("H", 0, 160), 0.0)
    fill(R("Q3"), 0.0)
    fill(R("XW", WX, GB), 0.0)
    fill(R("XW", BIGC, BIGC + 1), 1024.0)
    ts(R("UI"), R("PI"), 7, AND)
    ts(R("BI"), R("PI"), 3, SHR, 1, AND)
    ts(R("LI"), R("PI"), 15, AND)
    ts(R("UF"), R("UI"), 64.0, MUL)
    cp(R("BF"), R("BI"))
    ts(R("NBF"), R("BI"), -1.0, MUL, 1.0, ADD)
    ts(R("LF"), R("LI"), float(GB), ADD)
    tt(R("IB"), R("UF"), R("BF"), ADD)
    ts(R("IF"), R("A2"), R("IB"), ADD)
    ts(R("I8"), R("IF"), 8.0, MUL)
    ts(R("C37"), R("IF"), 37.0, MUL)
    ts(R("GK"), R("A2"), 8.0, MUL, R("LF"), ADD)
    for l in range(16):
        cp(R("LL", 128 * l + l, 128 * l + 128, 16), R("BGB", l, 128, 16))
    ts(R("NID"), R("IDN"), -1.0, MUL)
    ts(R("ID2"), R("IDN"), 2.0, MUL)
    fill(S("TF", 8), float(BIGC))
    ts(R("P5I"), R("PI"), 5, SHR)
    ts(R("S5"), R("P5I"), 1.0, EQ, -0.5, MUL)
    ts(R("P5"), R("P5I"), 2.0, EQ, -0.75, MUL)
    tt(R("AC"), R("S5"), R("P5"), ADD)
    ts(R("SCA"), R("AC"), 1.0, ADD)
    ts(R("NSCA"), R("AC"), -1.0, MUL, -1.0, ADD)
    tt(R("RRC"), R("RR2"), R("RR3"), ADD)
    ts(R("WF"), R("WI"), 0.5, MUL)
    ts(R("LW"), R("LL"), R("WF"), MUL)
    ts(R("ME"), R("M2", 0, 192, 2), R("NBF"), MUL)
    ts(R("MO"), R("M2", 1, 192, 2), R("BF"), MUL)
    tt(R("MNT"), R("ME"), R("MO"), ADD)
    cp(R("M"), S("MNT", 0))
    cp(R("NF"), S("MNT", 1))
    for s in range(2):
        ts(S("THH", s), S("MNT", 2), -1.0, MUL)
    for s in range(2):
        tt(R("IF"), S("THH", s), S("MNT", 2), ADD)
        ts(S("THL", s), R("IF"), -1.0, MUL)
    for s in range(8):
        ts(S("CUT", s), S("MNT", 1), float(s), LE, float(ZEROC if s == 0 else BIGC), MUL)
    tt(R("TF", 0, 256), R("TI"), R("CUT"), MAX)
    cp(R("TL0", 0, 256), R("TF", 0, 256))
    cp(R("H", 160, 416), R("HI"))

    dst_core = T.cores[(rank + 1) % n_ranks]
    src_core = T.cores[(rank - 1) % n_ranks]

    def lanes(a, b):
        return topo.engines(a, b)[:8]

    def ind(win, off):
        return lambda: ap(win).indirect(ap(off))

    def emit_gather_op(out, win, off, in1, op):
        w = ind(win, off)
        rec("v", lambda: g.vector.tensor_tensor(ap(out), w(), ap(in1), op), [win, off, in1], [out])

    TW = R("XW", 0, GB)
    for t in range(V):
        TL = "TL%d" % t
        n, M1, N8 = R("NF"), S("Q2", 3), S("Q1", 0)

        def transposed(q, bank, out):
            mms([(R(bank, 0, 128), R(q), R("IDN"))])
            act(R(out), R(bank, 0, 128), AF.Copy)

        def spread(bank, h, lhs, rhs, const=None):
            o = R(bank, 256 * h, 256 * h + 256)
            mms([(o, R(lhs), R(rhs))] + ([(o, R("IDN"), R(const))] if const else []))

        def gather_s(pair):
            o, lst = R("XT", 512 * pair[0], 512 * pair[-1] + 512), R(TL, 32 * pair[0], 32 * pair[-1] + 32)
            w = ind(TW, lst)
            rec("s", lambda: g.scalar.activation(ap(o), w(), AF.Copy), [TW, lst], [o])

        def first_card(t):
            if t == 0:
                cp(R("CDI"), R("C37"))
            else:
                ts(R("CDI"), R("C37"), R("AC"), ADD, float(613 * t), ADD)
            ts(R("MP"), R("M"), 0.0, GT)
            ts(R("CD"), R("CDI"), 4095, AND)
            ts(M1, R("M"), -1.0, ADD, 0.0, MAX)
            tt(R("DF"), S("H", 12 - t), R("CD"), SUB)
            tt(R("DF"), R("DF"), R("MP"), MUL)
            tt(R("CF"), R("DF"), R("CD"), ADD)
            cp(R("CU"), R("CF"))

        if t == 0:
            first_card(0)
        def xt(s):
            return R("XT", 512 * s, 512 * s + 512)

        def sub(s, bank):
            mms([(R(bank), R("IDN"), xt(s)), (R(bank), R("NID"), R("XC"))])

        def absv(s, bank=None):
            act(R("DA", 512 * s, 512 * s + 512), R(bank) if bank else xt(s), AF.Abs)

        def dist(s, bank, at):
            o = R(bank, at, at + 64)
            mms([(o, R("IDN"), R("THH")), (o, R("IDN"), R("THL"))]
                + [(o, R("LL", 128 * l, 128 * l + 128), R("DA", 512 * s + l, 512 * s + 1024, 16)) for l in range(16)])

        wc = ind(TW, R("CU"))
        rec("v", lambda wc=wc: g.vector.tensor_copy(ap(R("XC")), wc()), [TW, R("CU")], [R("XC")])
        gather_s([3, 4])
        gather_s([5])
        sub(3, "ps0")
        sub(4, "ps1")
        if t > 0:
            cp(n, R(TL, 256, NL))
        cp(S("Q1", 2), R("CF"))
        ts(N8, n, 1.0, ADD, 8.0, MIN)
        ts(S("Q1", 1), n, 8.0, GEQ)
        tt(R("FI"), M1, N8, ADD)
        tt(S("Q1", 3), R("CF"), S("Q1", 2), SUB)
        for b in range(3):
            ts(S("FB", b), R("FI"), 1 << b, AND)
        cp(R("Q2", 0, 96), R("FB"))
        if t > 0:
            cp(R("TF", 0, 256), R(TL, 0, 256))
            cp(R("A255"), R("AJ"))
        transposed("Q1", "ps6", "QT1")
        mms([(R("ps7", 0, 128), R("Q2"), R("IDN"))])
        act(R("QT2"), R("ps7", 0, 128), AF.Copy, scale=R("SCA"))
        act(R("QN2"), R("ps7", 0, 128), AF.Identity, bias=1.0, scale=R("NSCA"))
        spread("ps4", 1, "QT1", "RR0", "NSC")
        spread("ps4", 0, "QT1", "RR1")
        spread("ps5", 1, "QT2", "RR3")
        absv(3, "ps0")
        act(R("CNB"), R("ps4", 256, 512), AF.Abs, bias=-8192.0, scale=8192.0)
        sub(5, "ps0")
        spread("ps5", 0, "QT1", "RRC", "CNB")
        absv(4, "ps1")
        gather_s([6, 7])
        for b, bank in ((0, "ps6"), (1, "ps3"), (2, "ps7")):
            spread(bank, 0, "QT2", "RR%d" % b)
            spread(bank, 1, "QN2", "RR%d" % b)
        sub(6, "ps1")
        for s in VS:
            emit_gather_op(xt(s), TW, S(TL, s), R("XC"), SUB)

        tt(R("DSH"), R("TF", 32, 288), R("TF", 0, 256), SUB)
        tt(R("ps4", 0, 256), R("DSH"), R("ps4", 0, 256), MUL)
        tt(R("TS"), R("TF", 0, 256), R("ps4", 0, 256), ADD)
        tt(R("TS"), R("TS"), R("ps5", 0, 256), MIN)

        def rotate(src, dst, b, bank):
            k = 32 << b
            tt(R("B1", 0, 256 - k), R(src, k, 256), R(bank, 0, 256 - k), MUL)
            tt(R("B1", 256 - k, 256), R(src, 0, k), R(bank, 256 - k, 256), MUL)
            tt(R(bank, 256, 512), R(src), R(bank, 256, 512), MUL)
            tt(R(dst), R("B1"), R(bank, 256, 512), ADD)

        rotate("TS", "BA", 0, "ps6")
        rotate("BA", "BB", 1, "ps3")
        rotate("BB", "BA", 2, "ps7")
        hw = R("H", 32 * (4 - t), 32 * (12 - t))
        tt(R("ps5", 256, 512), R("SC7"), R("ps5", 256, 512), GEQ)
        tt(R("HD"), R("BA"), hw, SUB)
        tt(R("ps5", 256, 512), R("HD"), R("ps5", 256, 512), MUL)
        tt(hw, hw, R("ps5", 256, 512), ADD)

        absv(0)
        absv(1)
        dist(0, "ps2", 0)
        absv(5, "ps0")
        sub(7, "ps0")
        absv(2)
        dist(2, "ps2", 64)
        mms([(R("ps6"), R("ID2"), R("DA", 0, 512)), (R("ps6"), R("NID"), R("XC"))])
        dist(4, "ps2", 128)
        absv(6, "ps1")
        absv(7, "ps0")
        dist(6, "ps3", 0)
        act(R("XW", GB, WW), R("ps6"), AF.Identity, bias=0.5)
        act(R("XCM"), R("XC"), AF.Identity, bias=2047.5)

        tt(R("KEY"), R("TF", 0, 256), R("KC"), ADD)
        ts(R("V0"), S("TF", 0), 4096.0, LT)
        ts(R("N9"), n, 1.0, ADD)
        tt(S("KEY", 0), S("KEY", 0), R("V0"), MUL)
        lim = R("A255") if t else 0.0
        ts(R("ps2", 0, 192), R("ps2", 0, 192), lim, LE)
        tt(R("OKW"), R("KEY", 0, 192), R("ps2", 0, 192), MUL)
        tt(R("MX"), R("OKW", 0, 64), R("OKW", 64, 128), MAX)
        tt(S("MX", 0), S("MX", 0), R("GK"), MAX)
        tt(R("MX"), R("MX"), R("OKW", 128, 192), MAX)
        ts(R("ps3", 0, 64), R("ps3", 0, 64), lim, LE)
        tt(R("OKK"), R("KEY", 192, 256), R("ps3", 0, 64), MUL)
        tt(R("MX"), R("MX"), R("OKK"), MAX)
        tt(R("KI"), R("MX", 0, 32), R("MX", 32, 64), MAX)
        ts(R("KS"), R("KI"), 8191, AND)
        ts(R("K1"), R("KI"), 13, SHR)
        ts(S("Q3", 1), R("KI"), 8192.0, GEQ, 8192.0, MUL)
        cp(R("SU"), R("KS"))
        ts(S("Q3", 0), R("K1"), -1.0, ADD, 0.0, MAX)
        emit_gather_op(R("VV"), R("XW"), R("SU"), R("XCM"), ADD)
        transposed("Q3", "ps0", "QT3")
        spread("ps1", 0, "QT3", "RR0", "NSC")
        spread("ps1", 1, "QT3", "RR1")
        mms([(R("ps6", 0, 32), R("LW", 128 * l, 128 * l + 128), R("VV", l, 512, 16)) for l in range(16)])
        ts(R("HIT"), R("KI"), 8192.0, GEQ)
        tt(R("G1"), R("N9"), R("K1"), SUB)
        tt(R("N1"), N8, S("Q3", 1), SUB)
        ts(R("Y"), R("VV"), -2048.0, ADD, 0.5, MUL)
        tt(R("GOT"), R("G1"), R("HIT"), MUL)
        tt(R("NN"), R("N1"), S("Q3", 0), MAX)

        def train_out():
            act(R("ps1", 0, 256), R("ps1", 0, 256), AF.Relu, bias=float(BIGC), scale=-8192.0)
            tt(R("ps1", 256, 512), R("TS"), R("ps1", 256, 512), MAX)
            tt(R("X1"), R("TF", 0, 256), R("ps1", 0, 256), MAX)
            tt(R("TN"), R("X1"), R("ps1", 256, 512), MIN)

        def lengths():
            tt(R("MA"), M1, R("HIT"), ADD)
            tt(R("MB"), R("MA"), R("GOT"), ADD)
            ts(R("M"), R("MB"), 8.0, MIN)

        def scatter():
            wz = ind(R("XW", 0, WX), R("ZU"))
            rec("v", lambda: g.vector.tensor_copy(wz(), ap(R("Y"))), [R("Y"), R("ZU")], [R("XW", 0, WX)])

        def column():
            cp(R("ZI"), R("ps6", 0, 32))
            ts(R("ZJ"), R("ZI"), 7, AND)
            tt(R("ZF"), R("ZJ"), R("I8"), ADD)
            cp(R("ZU"), R("ZF"))

        if t < V - 1:
            TO, NX, tx, rx = "TO%d" % (t + 1), "TL%d" % (t + 1), "tx%d" % (t + 1), "rx%d" % (t + 1)
            cp(R(TO, 256, NL), R("NN"))
            lengths()
            train_out()
            ts(R(TO, 32, 256), R("TN", 32, 256), float(BIGC), MIN)
            ts(R(TO, 0, 32), R("TN", 0, 32), float(ZEROC), MIN)
            es = lanes(core, dst_core)
            rid, pid = topo.addr(dst_core)[:2]
            msk = sum(1 << e for e in es)
            rec("g", lambda TO=TO, NX=NX, tx=tx, rx=rx: g.remote_dma(T[NX][:, :], T[TO][:, :], T.sem[rx], T.sem[tx], pid, rid, msk),
                [R(TO)], [], tx, len(es))
            rec(None, None, [], [R(NX)], rx, len(lanes(src_core, core)))
            mms([(R("ps7", 0, 32), R("ONES"), R("GOT"))])
            column()
            rec("v", lambda: g.vector.tensor_reduce(T.AC[:, :], T.ps7[:, 0:32], AxisListType.X, ADD), [R("ps7", 0, 32)], [R("AC")])
            first_card(t + 1)
            scatter()
            cp(R("AI"), R("AC"))
            ts(R("AJ"), R("AI"), 255, AND)
        else:
            column()
            scatter()
            for f, gg, k in pieces:
                for h, q in enumerate(("y", "s")):
                    dma(q, "ox", T.yx[16 * gg:16 * (gg + k), 2048 * h:2048 * h + 2048], T.XW[16 * f:16 * (f + k), 2048 * h:2048 * h + 2048], [R("XW", 2048 * h, 2048 * h + 2048)], [])
            lengths()
            for nm, b in (("SEL0", 0), ("SEL1", 1)):
                for bb in range(2):
                    for gq in range(8):
                        cp(R(nm, 16 * gq + 8 * bb, 16 * gq + 8 * bb + 8), R("IDN", 16 * gq + 8 * b, 16 * gq + 8 * b + 8))
            cp(S("MNB", 0), R("M"))
            cp(S("MNB", 1), R("NN"))
            mms([(R("ps7", 0, 64), R("SEL0"), R("MNB"))])
            mms([(R("ps7", 64, 128), R("SEL1"), R("MNB"))])
            for b in range(2):
                cp(R("YMB", b, 64, 2), R("ps7", 64 * b, 64 * b + 32))
                cp(R("YNB", b, 64, 2), R("ps7", 64 * b + 32, 64 * b + 64))
            dma("y", "om1", T.DYm[:, :], T.YMB[:, :], [R("YMB")], [R("DYm")])
            dma("y", "om1", T.DYn[:, :], T.YNB[:, :], [R("YNB")], [R("DYn")])
            train_out()
            ts(R("OG"), R("TN"), 4096.0, LT)
            tt(R("OT"), R("TN"), R("OG"), MUL)
            for s in range(8):
                for f, gg, k in pieces:
                    dma("s", "ot", T.yt[16 * gg + s:16 * (gg + k):8, :], T.OT[16 * f:16 * (f + k), 32 * s:32 * s + 32], [S("OT", s)], [])
            for s in range(8):
                ts(S("OG", 7 - s), R("M"), float(s), GT)
            tt(R("OH"), R("OG"), R("H", 0, 256), MUL)
            for s in range(8):
                for f, gg, k in pieces:
                    dma("y" if s % 2 else "s", "oh", T.yh[16 * gg + s:16 * (gg + k):8, :], T.OH[16 * f:16 * (f + k), 32 * (7 - s):32 * (8 - s)], [S("OH", 7 - s)], [])
            for f, gg, k in pieces:
                dma("y", "om2", T.ym[gg:gg + k, :], T.DYm[f:f + k, 0:512], [R("DYm")], [])
                dma("y", "om2", T.yn[gg:gg + k, :], T.DYn[f:f + k, 0:512], [R("DYn")], [])

    emit(ops, queues, T)


def emit(ops, queues, T):
    hist = {}
    know = {q: {} for q in queues}
    clk, total = [], {}
    waits, needed = [], [False] * len(ops)
    gclk = {}

    def merge(a, b):
        for k in b:
            if b[k] > a.get(k, -1):
                a[k] = b[k]

    for i, o in enumerate(ops):
        q, deps = o["q"], []
        me = o["grp"] or q
        acc = [(r, False) for r in o["r"]] + [(w, True) for w in o["w"]]
        for (nm, lo, hi, st), wr in acc:
            bank = nm.startswith("ps")
            for (l2, h2, j, w2) in hist.get(nm, []):
                who = ops[j]["grp"] or ops[j]["q"]
                if l2 < hi and lo < h2 or (bank and who != me):
                    if who == me and o["grp"]:
                        continue
                    if w2 or wr or (bank and who != me):
                        deps.append(j)
        wl = []
        c = {}
        if q is not None:
            k = know[q]
            for j in sorted(set(deps), reverse=True):
                oj = ops[j]
                if oj["grp"]:
                    if k.get(oj["grp"], -1) >= 0:
                        continue
                    wl.append(("grp", oj["grp"]))
                    k[oj["grp"]] = 0
                    merge(k, gclk[oj["grp"]])
                else:
                    if k.get(oj["q"], -1) >= j:
                        continue
                    wl.append(("op", j))
                    needed[j] = True
                    merge(k, clk[j])
            c = dict(k)
        if o["grp"]:
            total[o["grp"]] = total.get(o["grp"], 0) + o["inc"]
            merge(gclk.setdefault(o["grp"], {}), c)
        else:
            c[q] = i
        clk.append(c)
        waits.append(wl)
        for (nm, lo, hi, st), wr in acc:
            lst = hist.setdefault(nm, [])
            if wr and st == 1:
                lst[:] = [e for e in lst if not (lo <= e[0] and e[1] <= hi) or (o["grp"] and (ops[e[2]]["grp"] == o["grp"]))]
            lst.append((lo, hi, i, wr))
    count, rank_in = {q: 0 for q in queues}, {}
    waited = set()
    for i, o in enumerate(ops):
        q = o["q"]
        if q is None:
            continue
        best = {}
        for kind, x in waits[i]:
            if kind == "grp":
                best[x] = total[x]
                waited.add(x)
            else:
                sn = "e_" + ops[x]["q"]
                best[sn] = max(best.get(sn, 0), rank_in[x])
        for sn in best:
            queues[q].wait_ge(T.sem[sn], best[sn])
        inst = o["fn"]()
        if o["grp"]:
            if not o["grp"].startswith("tx"):
                inst.then_inc(T.sem[o["grp"]], 16)
        elif needed[i]:
            count[q] += 1
            rank_in[i] = count[q]
            inst.then_inc(T.sem["e_" + q], 1)
    for x in total:
        if x not in waited:
            (queues["g"] if x.startswith("tx") else queues["y"]).wait_ge(T.sem[x], total[x])
